import numpy as np
import ml_dtypes


def mxq(x, axis, fmt="e4m3"):
    dtype, down = {"e4m3": (ml_dtypes.float8_e4m3fn, 7), "e5m2": (ml_dtypes.float8_e5m2, 14)}[fmt]
    v = np.moveaxis(np.asarray(x, np.float32).astype(ml_dtypes.bfloat16).astype(np.float64), axis, -1)
    blocks = v.reshape(v.shape[:-1] + (-1, 32))
    amax = np.abs(blocks).max(-1, keepdims=True)
    byte = np.maximum(np.where(amax > 0, np.frexp(amax)[1] - 1 + 127, 0) - down, 1)
    scale = np.exp2(byte - 127.0)
    codes = (blocks / scale).astype(np.float32).astype(dtype).astype(np.float64)
    return np.moveaxis((codes * scale).reshape(v.shape), -1, axis)


WIDE = False


def mx_kscale(k):
    if not WIDE:
        return np.ones(k)
    levels = np.array([10, -10, 5, -5, 0])
    if k % 512:
        return np.exp2(np.random.permutation(np.resize(levels, k // 32))).repeat(32)
    a = np.empty((k // 512, 16))
    for p in range(k // 512):
        a[p, :8] = np.random.permutation(np.resize(levels, 8))
        for g in range(8):
            far = levels[np.abs(levels - a[p, g]) >= 10]
            a[p, g + 8] = far[np.random.randint(len(far))]
    return np.exp2(a.ravel()).repeat(32)


def f64(x):
    return np.asarray(x).astype(np.float64)


def striped(idx):
    return np.tile(idx.reshape(-1, 16).T, (8, 1)).astype(np.uint16)


def unstriped(offs):
    return offs[:16].T.reshape(-1).astype(np.int64)


def silu(v):
    return v / (1.0 + np.exp(-np.maximum(v, -700.0)))


K, T, E, C, N = 1024, 768, 6, 256, 128


def by_expert(wq, xq):
    return np.concatenate([wq[e].T @ xq[:, e * C:(e + 1) * C] for e in range(E)], axis=1)


def setup_inputs():
    n = np.random.standard_normal
    s = mx_kscale(K)[:, None]
    first = np.random.permutation(np.repeat(np.arange(E), T // E))
    second = (first + 1 + np.random.permutation(np.repeat(np.arange(E - 1), -(-T // (E - 1)))[:T])) % E
    while np.bincount(second, minlength=E).max() != T // E:
        load = np.bincount(second, minlength=E); hi, lo = int(load.argmax()), int(load.argmin())
        t = np.flatnonzero((second == hi) & (first != lo))[0]; second[t] = lo
    slot_token = np.empty(E * C, np.int64); pos = np.empty((2, T), np.int64); fill = np.zeros(E, np.int64)
    place = np.stack([np.random.permutation(C) for _ in range(E)])
    for r, deal in enumerate((first, second)):
        for t in np.random.permutation(T):
            e = deal[t]; j = e * C + place[e, fill[e]]; fill[e] += 1; slot_token[j] = t; pos[r, t] = j
    g = np.random.uniform(0.2, 0.8, T)
    return {
        "xT": (n((K, T)) * s).astype(np.float32),
        "w": (n((E + 1, K, N)) / np.sqrt(K) / s[None]).astype(np.float32),
        "b": (0.3 * n((N, E + 1))).astype(np.float32),
        "gate": np.stack([np.tile(g, (N, 1)), np.tile(1.0 - g, (N, 1))]).astype(np.float32),
        "offs": striped(slot_token),
        "pos1": striped(pos[0]),
        "pos2": striped(pos[1]),
    }


def reference(xT, w, b, gate, offs, pos1, pos2):
    idx = unstriped(offs)
    wq = mxq(f64(w), 1, "e4m3")
    xs = mxq(f64(xT), 0, "e4m3")
    ys = silu((wq[E].T @ xs) + f64(b)[:, E:])
    xq = mxq(f64(xT)[:, idx], 0, "e4m3")
    y = by_expert(wq, xq)
    y = silu(y + np.repeat(f64(b)[:, :E], C, axis=1))
    return ys + f64(gate[0]) * y[:, unstriped(pos1)] + f64(gate[1]) * y[:, unstriped(pos2)]

@@ -1,0 +1,218 @@
+from contextlib import ExitStack
+
+import concourse.mybir as mybir
+
+K, T, E, C, N = 1024, 768, 6, 256, 128
+S = E * C
+P = 128
+GROUPS = K // 512
+FLOPS = 2 * K * N * (S + T)
+
+F32 = mybir.dt.float32
+BF16 = mybir.dt.bfloat16
+U32 = mybir.dt.uint32
+U16 = mybir.dt.uint16
+U8 = mybir.dt.uint8
+FP8X4 = mybir.dt.float8_e4m3fn_x4
+ADD = mybir.AluOpType.add
+MULT = mybir.AluOpType.mult
+SILU = mybir.ActivationFunctionType.Silu
+
+CUT = 512
+CUTS = S // CUT
+HALF = T // 2
+
+
+def tile_moe_shr_lin_silu_kernel(tc, xT, w, b, gate, offs, pos1, pos2, out):
+    nc = tc.nc
+    with ExitStack() as ctx:
+        keep = ctx.enter_context(tc.tile_pool(name="keep", bufs=1))
+        psum = ctx.enter_context(tc.psum_pool(name="psum", bufs=1))
+
+        offs_sb = keep.tile([P, S // 16], U16, name="offs_sb")
+        pos1_sb = keep.tile([P, T // 16], U16, name="pos1_sb")
+        pos2_sb = keep.tile([P, T // 16], U16, name="pos2_sb")
+        b_sb = keep.tile([P, E + 1], F32, name="b_sb")
+        gate_sb = [keep.tile([P, T], F32, name=f"gate{r}") for r in range(2)]
+        x_raw = [keep.tile([P, 4, T], F32, name=f"x_raw{g}") for g in range(GROUPS)]
+        w_raw = [keep.tile([P, GROUPS, 4, N], F32, name=f"w_raw{e}") for e in range(E + 1)]
+        pairs = [[keep.tile([P, T, 2], BF16, name=f"pairs{g}{u}") for u in range(2)] for g in range(GROUPS)]
+        picked = [keep.tile([P, 2, S, 2], BF16, name=f"picked{g}") for g in range(GROUPS)]
+        slots = [keep.tile([P, S, 4], BF16, align_bytes=64, name=f"slots{g}") for g in range(GROUPS)]
+        slot_codes = [keep.tile([P, S], U32, align_bytes=64, name=f"slot_codes{g}") for g in range(GROUPS)]
+        slot_scales = [keep.tile([P, S], U8, align_bytes=64, name=f"slot_scales{g}") for g in range(GROUPS)]
+        toks = [keep.tile([P, T, 4], BF16, align_bytes=64, name=f"toks{g}") for g in range(GROUPS)]
+        tok_codes = [keep.tile([P, T], U32, align_bytes=64, name=f"tok_codes{g}") for g in range(GROUPS)]
+        tok_scales = [keep.tile([P, T], U8, align_bytes=64, name=f"tok_scales{g}") for g in range(GROUPS)]
+        w_bf = [keep.tile([P, GROUPS, N, 4], BF16, align_bytes=64, name=f"w_bf{e}") for e in range(E + 1)]
+        w_codes = [keep.tile([P, GROUPS, N], U32, align_bytes=64, name=f"w_codes{e}") for e in range(E + 1)]
+        w_scales = [keep.tile([P, GROUPS, N], U8, align_bytes=64, name=f"w_scales{e}") for e in range(E + 1)]
+        y = keep.tile([P, S], F32, name="y")
+        ys = keep.tile([P, T], F32, name="ys")
+        warm = keep.tile([P, 1], F32, name="warm")
+        acc = [psum.tile([P, C], F32, name=f"acc{e}") for e in range(E)]
+        acc_s = [psum.tile([P, n], F32, name=f"acc_s{n}") for n in (512, 256)]
+
+        nc.sync.dma_start(out=offs_sb[:], in_=offs)
+        x_rows = xT.rearrange("(g p j) t -> g p j t", g=GROUPS, j=4)
+        w_rows = w.rearrange("e (g p j) n -> e p g j n", g=GROUPS, j=4)
+        for g in range(GROUPS):
+            for u in range(2):
+                nc.sync.dma_start(out=x_raw[g][:, 2 * u : 2 * u + 2, :], in_=x_rows[g, :, 2 * u : 2 * u + 2, :])
+        for e in range(E + 1):
+            for g in range(GROUPS):
+                nc.sync.dma_start(out=w_raw[e][:, g], in_=w_rows[e, :, g])
+            if e == 0:
+                nc.sync.dma_start(out=b_sb[:], in_=b)
+        nc.sync.dma_start(out=pos1_sb[:], in_=pos1)
+        nc.sync.dma_start(out=pos2_sb[:], in_=pos2)
+        for r in range(2):
+            nc.sync.dma_start(out=gate_sb[r][:], in_=gate[r])
+
+        nc.vector.memset(warm[:], 0.0)
+        nc.scalar.activation(warm[:], warm[:], SILU)
+
+        def make_pairs(copy, g, u, a, z):
+            copy(out=pairs[g][u][:, a:z, :], in_=x_raw[g][:, 2 * u : 2 * u + 2, a:z].rearrange("p t n -> p n t"))
+
+        def pick(g, u, i):
+            s = slice(i * CUT, (i + 1) * CUT)
+            window = pairs[g][u][:].rearrange("p n t -> p (n t)").bitcast(U32)
+            into = picked[g][:, u, s, :].rearrange("p s t -> p (s t)").bitcast(U32)
+            nc.vector.tensor_copy(into, window.indirect(offs_sb[:, i * CUT // 16 : (i + 1) * CUT // 16]))
+
+        def weave(g, i):
+            s = slice(i * CUT, (i + 1) * CUT)
+            nc.vector.tensor_copy(
+                out=slots[g][:, s, :].rearrange("p s (u t) -> p s u t", t=2),
+                in_=picked[g][:, :, s, :].rearrange("p u s t -> p s u t"),
+            )
+
+        def quantise_slots(g, i):
+            s = slice(i * CUT, (i + 1) * CUT)
+            nc.vector.quantize_mx(
+                out=slot_codes[g][:, s].bitcast(FP8X4),
+                scales=slot_scales[g][:, s],
+                in_=slots[g][:, s, :].rearrange("p s t -> p (s t)"),
+            )
+
+        def spread_w(copy, e):
+            for g in range(GROUPS):
+                copy(
+                    out=w_bf[e][:, g].rearrange("p (c i) t -> p c t i", i=4),
+                    in_=w_raw[e][:, g].rearrange("p t (c i) -> p c t i", i=4),
+                )
+
+        def quantise_w(e):
+            nc.vector.quantize_mx(
+                out=w_codes[e][:].rearrange("p g n -> p (g n)").bitcast(FP8X4),
+                scales=w_scales[e][:].rearrange("p g n -> p (g n)"),
+                in_=w_bf[e][:].rearrange("p g n t -> p (g n t)"),
+            )
+
+        def spread_toks(copy, g, a, z):
+            copy(
+                out=toks[g][:, a:z, :].rearrange("p (c i) t -> p c t i", i=4),
+                in_=x_raw[g][:, :, a:z].rearrange("p t (c i) -> p c t i", i=4),
+            )
+
+        def quantise_toks(g, a, z):
+            nc.vector.quantize_mx(
+                out=tok_codes[g][:, a:z].bitcast(FP8X4),
+                scales=tok_scales[g][:, a:z],
+                in_=toks[g][:, a:z, :].rearrange("p s t -> p (s t)"),
+            )
+
+        def multiply(bank, e, g, codes, scales, cols):
+            nc.tensor.matmul_mx(
+                out=bank,
+                lhsT=w_codes[e][:, g].bitcast(FP8X4),
+                lhsT_scale=w_scales[e][:, g],
+                rhs=codes[g][:, cols].bitcast(FP8X4),
+                rhs_scale=scales[g][:, cols],
+                start=(g == 0),
+                stop=(g == GROUPS - 1),
+            )
+
+        def experts(g, i):
+            for e in (2 * i, 2 * i + 1):
+                multiply(acc[e][:], e, g, slot_codes, slot_scales, slice(e * C, (e + 1) * C))
+
+        def finish(i):
+            for e in (2 * i, 2 * i + 1):
+                nc.scalar.activation(y[:, e * C : (e + 1) * C], acc[e][:], SILU, bias=b_sb[:, e : e + 1])
+
+        V, A = nc.vector.tensor_copy, nc.scalar.copy
+        make_pairs(V, 0, 0, 0, HALF)
+        make_pairs(A, 0, 0, HALF, T)
+        for i in range(CUTS):
+            pick(0, 0, i)
+        make_pairs(A, 0, 1, 0, T)
+        make_pairs(A, 1, 0, 0, T)
+        make_pairs(A, 1, 1, 0, T)
+        pick(0, 1, 0)
+        pick(0, 1, 1)
+        weave(0, 0)
+        pick(0, 1, 2)
+        quantise_slots(0, 0)
+        weave(0, 1)
+        spread_w(A, 0)
+        spread_w(A, 1)
+        pick(1, 0, 0)
+        quantise_slots(0, 1)
+        weave(0, 2)
+        pick(1, 0, 1)
+        quantise_slots(0, 2)
+        spread_w(A, 2)
+        spread_w(A, 3)
+        pick(1, 0, 2)
+        quantise_w(0)
+        quantise_w(1)
+        experts(0, 0)
+        pick(1, 1, 0)
+        quantise_w(2)
+        quantise_w(3)
+        experts(0, 1)
+        spread_w(A, 4)
+        spread_w(A, 5)
+        weave(1, 0)
+        pick(1, 1, 1)
+        quantise_slots(1, 0)
+        experts(1, 0)
+        quantise_w(4)
+        quantise_w(5)
+        experts(0, 2)
+        finish(0)
+        spread_w(A, 6)
+        spread_toks(A, 0, 0, 512)
+        spread_toks(A, 0, 512, T)
+        spread_toks(A, 1, 0, 512)
+        spread_toks(A, 1, 512, T)
+        weave(1, 1)
+        pick(1, 1, 2)
+        quantise_slots(1, 1)
+        experts(1, 1)
+        finish(1)
+        weave(1, 2)
+        quantise_w(6)
+        quantise_slots(1, 2)
+        experts(1, 2)
+        finish(2)
+        for h, (a, z) in enumerate(((0, 512), (512, T))):
+            for g in range(GROUPS):
+                quantise_toks(g, a, z)
+                multiply(acc_s[h][:], E, g, tok_codes, tok_scales, slice(a, z))
+            nc.scalar.activation(ys[:, a:z], acc_s[h][:], SILU, bias=b_sb[:, E : E + 1])
+
+        for h in range(2):
+            s = slice(h * HALF, (h + 1) * HALF)
+            o = slice(h * HALF // 16, (h + 1) * HALF // 16)
+            first = keep.tile([P, HALF], F32, name=f"first{h}")
+            second = keep.tile([P, HALF], F32, name=f"second{h}")
+            both = keep.tile([P, HALF], F32, name=f"both{h}")
+            total = keep.tile([P, HALF], F32, name=f"total{h}")
+            nc.vector.tensor_tensor(first[:], y[:].indirect(pos1_sb[:, o]), gate_sb[0][:, s], MULT)
+            nc.vector.tensor_tensor(second[:], y[:].indirect(pos2_sb[:, o]), gate_sb[1][:, s], MULT)
+            nc.vector.tensor_tensor(both[:], first[:], ys[:, s], ADD)
+            nc.vector.tensor_tensor(total[:], both[:], second[:], ADD)
+            nc.sync.dma_start(out=out[:, s], in_=total[:])

@@ -36,17 +36,17 @@ def tile_moe_shr_lin_silu_kernel(tc, xT, w, b, gate, offs, pos1, pos2, out):
         gate_sb = [keep.tile([P, T], F32, name=f"gate{r}") for r in range(2)]
         x_raw = [keep.tile([P, 4, T], F32, name=f"x_raw{g}") for g in range(GROUPS)]
         w_raw = [keep.tile([P, GROUPS, 4, N], F32, name=f"w_raw{e}") for e in range(E + 1)]
-        pairs = [[keep.tile([P, T, 2], BF16, name=f"pairs{g}{u}") for u in range(2)] for g in range(GROUPS)]
+        pairs = [keep.tile([P, 2, T, 2], BF16, name=f"pairs{g}") for g in range(GROUPS)]
         picked = [keep.tile([P, 2, S, 2], BF16, name=f"picked{g}") for g in range(GROUPS)]
         slots = [keep.tile([P, S, 4], BF16, align_bytes=64, name=f"slots{g}") for g in range(GROUPS)]
         slot_codes = [keep.tile([P, S], U32, align_bytes=64, name=f"slot_codes{g}") for g in range(GROUPS)]
         slot_scales = [keep.tile([P, S], U8, align_bytes=64, name=f"slot_scales{g}") for g in range(GROUPS)]
-        toks = [keep.tile([P, T, 4], BF16, align_bytes=64, name=f"toks{g}") for g in range(GROUPS)]
-        tok_codes = [keep.tile([P, T], U32, align_bytes=64, name=f"tok_codes{g}") for g in range(GROUPS)]
-        tok_scales = [keep.tile([P, T], U8, align_bytes=64, name=f"tok_scales{g}") for g in range(GROUPS)]
-        w_bf = [keep.tile([P, GROUPS, N, 4], BF16, align_bytes=64, name=f"w_bf{e}") for e in range(E + 1)]
-        w_codes = [keep.tile([P, GROUPS, N], U32, align_bytes=64, name=f"w_codes{e}") for e in range(E + 1)]
-        w_scales = [keep.tile([P, GROUPS, N], U8, align_bytes=64, name=f"w_scales{e}") for e in range(E + 1)]
+        toks = keep.tile([P, GROUPS * T, 4], BF16, align_bytes=64, name="toks")
+        tok_codes = keep.tile([P, GROUPS * T], U32, align_bytes=64, name="tok_codes")
+        tok_scales = keep.tile([P, GROUPS * T], U8, align_bytes=64, name="tok_scales")
+        w_bf = keep.tile([P, (E + 1) * GROUPS * N, 4], BF16, align_bytes=64, name="w_bf")
+        w_codes = keep.tile([P, (E + 1) * GROUPS * N], U32, align_bytes=64, name="w_codes")
+        w_scales = keep.tile([P, (E + 1) * GROUPS * N], U8, align_bytes=64, name="w_scales")
         y = keep.tile([P, S], F32, name="y")
         ys = keep.tile([P, T], F32, name="ys")
         warm = keep.tile([P, 1], F32, name="warm")
@@ -58,12 +58,11 @@ def tile_moe_shr_lin_silu_kernel(tc, xT, w, b, gate, offs, pos1, pos2, out):
         w_rows = w.rearrange("e (g p j) n -> e p g j n", g=GROUPS, j=4)
         for g in range(GROUPS):
             for u in range(2):
-                nc.sync.dma_start(out=x_raw[g][:, 2 * u : 2 * u + 2, :], in_=x_rows[g, :, 2 * u : 2 * u + 2, :])
+                for a, z in ((0, HALF), (HALF, T)) if g + u == 0 else ((0, T),):
+                    nc.sync.dma_start(out=x_raw[g][:, 2 * u : 2 * u + 2, a:z], in_=x_rows[g, :, 2 * u : 2 * u + 2, a:z])
         for e in range(E + 1):
-            for g in range(GROUPS):
-                nc.sync.dma_start(out=w_raw[e][:, g], in_=w_rows[e, :, g])
-            if e == 0:
-                nc.sync.dma_start(out=b_sb[:], in_=b)
+            nc.sync.dma_start(out=w_raw[e][:], in_=w_rows[e])
+        nc.sync.dma_start(out=b_sb[:], in_=b)
         nc.sync.dma_start(out=pos1_sb[:], in_=pos1)
         nc.sync.dma_start(out=pos2_sb[:], in_=pos2)
         for r in range(2):
@@ -73,146 +72,128 @@ def tile_moe_shr_lin_silu_kernel(tc, xT, w, b, gate, offs, pos1, pos2, out):
         nc.scalar.activation(warm[:], warm[:], SILU)
 
         def make_pairs(copy, g, u, a, z):
-            copy(out=pairs[g][u][:, a:z, :], in_=x_raw[g][:, 2 * u : 2 * u + 2, a:z].rearrange("p t n -> p n t"))
+            copy(out=pairs[g][:, u, a:z, :], in_=x_raw[g][:, 2 * u : 2 * u + 2, a:z].rearrange("p t n -> p n t"))
 
         def pick(g, u, i):
             s = slice(i * CUT, (i + 1) * CUT)
-            window = pairs[g][u][:].rearrange("p n t -> p (n t)").bitcast(U32)
+            window = pairs[g][:, u].rearrange("p n t -> p (n t)").bitcast(U32)
             into = picked[g][:, u, s, :].rearrange("p s t -> p (s t)").bitcast(U32)
             nc.vector.tensor_copy(into, window.indirect(offs_sb[:, i * CUT // 16 : (i + 1) * CUT // 16]))
 
-        def weave(g, i):
-            s = slice(i * CUT, (i + 1) * CUT)
-            nc.vector.tensor_copy(
-                out=slots[g][:, s, :].rearrange("p s (u t) -> p s u t", t=2),
-                in_=picked[g][:, :, s, :].rearrange("p u s t -> p s u t"),
+        def weave(copy, into, b0, planes, a, z):
+            copy(
+                out=into[:, b0 + a : b0 + z, :].rearrange("p s t -> p (s t)").bitcast(F32).rearrange("p (s u) -> p s u", u=2),
+                in_=planes[:].rearrange("p u s t -> p (u s t)").bitcast(F32).rearrange("p (u s) -> p s u", u=2)[:, a:z, :],
             )
 
-        def quantise_slots(g, i):
-            s = slice(i * CUT, (i + 1) * CUT)
+        def quantise(values, codes, scales, a, z):
             nc.vector.quantize_mx(
-                out=slot_codes[g][:, s].bitcast(FP8X4),
-                scales=slot_scales[g][:, s],
-                in_=slots[g][:, s, :].rearrange("p s t -> p (s t)"),
+                out=codes[:, a:z].bitcast(FP8X4),
+                scales=scales[:, a:z],
+                in_=values[:, a:z, :].rearrange("p s t -> p (s t)"),
             )
+
+        def quantise_slots(g, a, z):
+            quantise(slots[g], slot_codes[g], slot_scales[g], a, z)
+
+        def quantise_w(a, z):
+            quantise(w_bf, w_codes, w_scales, a * GROUPS * N, z * GROUPS * N)
 
         def spread_w(copy, e):
-            for g in range(GROUPS):
-                copy(
-                    out=w_bf[e][:, g].rearrange("p (c i) t -> p c t i", i=4),
-                    in_=w_raw[e][:, g].rearrange("p t (c i) -> p c t i", i=4),
-                )
-
-        def quantise_w(e):
-            nc.vector.quantize_mx(
-                out=w_codes[e][:].rearrange("p g n -> p (g n)").bitcast(FP8X4),
-                scales=w_scales[e][:].rearrange("p g n -> p (g n)"),
-                in_=w_bf[e][:].rearrange("p g n t -> p (g n t)"),
-            )
-
-        def spread_toks(copy, g, a, z):
+            c = e * GROUPS * N
             copy(
-                out=toks[g][:, a:z, :].rearrange("p (c i) t -> p c t i", i=4),
-                in_=x_raw[g][:, :, a:z].rearrange("p t (c i) -> p c t i", i=4),
-            )
-
-        def quantise_toks(g, a, z):
-            nc.vector.quantize_mx(
-                out=tok_codes[g][:, a:z].bitcast(FP8X4),
-                scales=tok_scales[g][:, a:z],
-                in_=toks[g][:, a:z, :].rearrange("p s t -> p (s t)"),
+                out=w_bf[:, c : c + GROUPS * N, :].rearrange("p (g c i) t -> p g c t i", g=GROUPS, i=4),
+                in_=w_raw[e][:].rearrange("p g t (c i) -> p g c t i", i=4),
             )
 
         def multiply(bank, e, g, codes, scales, cols):
+            c = slice((e * GROUPS + g) * N, (e * GROUPS + g + 1) * N)
             nc.tensor.matmul_mx(
                 out=bank,
-                lhsT=w_codes[e][:, g].bitcast(FP8X4),
-                lhsT_scale=w_scales[e][:, g],
-                rhs=codes[g][:, cols].bitcast(FP8X4),
-                rhs_scale=scales[g][:, cols],
+                lhsT=w_codes[:, c].bitcast(FP8X4),
+                lhsT_scale=w_scales[:, c],
+                rhs=codes[:, cols].bitcast(FP8X4),
+                rhs_scale=scales[:, cols],
                 start=(g == 0),
                 stop=(g == GROUPS - 1),
             )
 
-        def experts(g, i):
-            for e in (2 * i, 2 * i + 1):
-                multiply(acc[e][:], e, g, slot_codes, slot_scales, slice(e * C, (e + 1) * C))
-
-        def finish(i):
-            for e in (2 * i, 2 * i + 1):
-                nc.scalar.activation(y[:, e * C : (e + 1) * C], acc[e][:], SILU, bias=b_sb[:, e : e + 1])
+        def expert(e):
+            s = slice(e * C, (e + 1) * C)
+            for g in range(GROUPS):
+                multiply(acc[e][:], e, g, slot_codes[g], slot_scales[g], s)
+            nc.scalar.activation(y[:, s], acc[e][:], SILU, bias=b_sb[:, e : e + 1])
 
         V, A = nc.vector.tensor_copy, nc.scalar.copy
-        make_pairs(V, 0, 0, 0, HALF)
-        make_pairs(A, 0, 0, HALF, T)
+        make_pairs(A, 0, 0, 0, HALF)
+        make_pairs(V, 0, 0, HALF, T)
         for i in range(CUTS):
             pick(0, 0, i)
         make_pairs(A, 0, 1, 0, T)
         make_pairs(A, 1, 0, 0, T)
         make_pairs(A, 1, 1, 0, T)
-        pick(0, 1, 0)
-        pick(0, 1, 1)
-        weave(0, 0)
-        pick(0, 1, 2)
-        quantise_slots(0, 0)
-        weave(0, 1)
+        for i in range(CUTS):
+            pick(0, 1, i)
         spread_w(A, 0)
-        spread_w(A, 1)
+        weave(A, slots[0], 0, picked[0], 0, 1024)
+        weave(A, slots[0], 0, picked[0], 1024, S)
         pick(1, 0, 0)
-        quantise_slots(0, 1)
-        weave(0, 2)
+        pick(1, 1, 0)
+        for e in range(1, 3):
+            spread_w(A, e)
+        quantise_slots(0, 0, 1024)
         pick(1, 0, 1)
-        quantise_slots(0, 2)
-        spread_w(A, 2)
+        quantise_slots(0, 1024, S)
+        pick(1, 1, 1)
+        weave(A, slots[1], 0, picked[1], 0, 512)
         spread_w(A, 3)
         pick(1, 0, 2)
-        quantise_w(0)
-        quantise_w(1)
-        experts(0, 0)
-        pick(1, 1, 0)
-        quantise_w(2)
-        quantise_w(3)
-        experts(0, 1)
-        spread_w(A, 4)
-        spread_w(A, 5)
-        weave(1, 0)
-        pick(1, 1, 1)
-        quantise_slots(1, 0)
-        experts(1, 0)
-        quantise_w(4)
-        quantise_w(5)
-        experts(0, 2)
-        finish(0)
-        spread_w(A, 6)
-        spread_toks(A, 0, 0, 512)
-        spread_toks(A, 0, 512, T)
-        spread_toks(A, 1, 0, 512)
-        spread_toks(A, 1, 512, T)
-        weave(1, 1)
         pick(1, 1, 2)
-        quantise_slots(1, 1)
-        experts(1, 1)
-        finish(1)
-        weave(1, 2)
-        quantise_w(6)
-        quantise_slots(1, 2)
-        experts(1, 2)
-        finish(2)
+        for e in range(4, E + 1):
+            spread_w(A, e)
+        weave(A, toks, 0, pairs[0], 0, T)
+        weave(A, toks, T, pairs[1], 0, T)
+        weave(V, slots[1], 0, picked[1], 512, 1024)
+        quantise_w(0, 4)
+        quantise_slots(1, 0, 1024)
+        for e in range(4):
+            expert(e)
+        weave(V, slots[1], 0, picked[1], 1024, S)
+        quantise_w(4, E)
+        quantise_slots(1, 1024, S)
+        for e in range(4, E):
+            expert(e)
+        quantise(toks, tok_codes, tok_scales, 0, 1024)
+        quantise(toks, tok_codes, tok_scales, 1024, GROUPS * T)
+        quantise_w(E, E + 1)
         for h, (a, z) in enumerate(((0, 512), (512, T))):
             for g in range(GROUPS):
-                quantise_toks(g, a, z)
-                multiply(acc_s[h][:], E, g, tok_codes, tok_scales, slice(a, z))
+                multiply(acc_s[h][:], E, g, tok_codes, tok_scales, slice(g * T + a, g * T + z))
             nc.scalar.activation(ys[:, a:z], acc_s[h][:], SILU, bias=b_sb[:, E : E + 1])
 
-        for h in range(2):
-            s = slice(h * HALF, (h + 1) * HALF)
-            o = slice(h * HALF // 16, (h + 1) * HALF // 16)
-            first = keep.tile([P, HALF], F32, name=f"first{h}")
-            second = keep.tile([P, HALF], F32, name=f"second{h}")
-            both = keep.tile([P, HALF], F32, name=f"both{h}")
-            total = keep.tile([P, HALF], F32, name=f"total{h}")
-            nc.vector.tensor_tensor(first[:], y[:].indirect(pos1_sb[:, o]), gate_sb[0][:, s], MULT)
-            nc.vector.tensor_tensor(second[:], y[:].indirect(pos2_sb[:, o]), gate_sb[1][:, s], MULT)
-            nc.vector.tensor_tensor(both[:], first[:], ys[:, s], ADD)
-            nc.vector.tensor_tensor(total[:], both[:], second[:], ADD)
-            nc.sync.dma_start(out=out[:, s], in_=total[:])
+        bounds = ((0, 512), (512, T))
+        parts = []
+        for h, (a, z) in enumerate(bounds):
+            parts.append([keep.tile([P, z - a], F32, name=f"part{h}{k}") for k in range(4)])
+
+        def pick_result(h, r, pos_sb):
+            a, z = bounds[h]
+            nc.vector.tensor_tensor(parts[h][r][:], y[:].indirect(pos_sb[:, a // 16 : z // 16]), gate_sb[r][:, a:z], MULT)
+
+        def add_shared(h):
+            a, z = bounds[h]
+            nc.vector.tensor_tensor(parts[h][2][:], parts[h][0][:], ys[:, a:z], ADD)
+
+        def add_second(h):
+            a, z = bounds[h]
+            nc.vector.tensor_tensor(parts[h][3][:], parts[h][2][:], parts[h][1][:], ADD)
+            nc.sync.dma_start(out=out[:, a:z], in_=parts[h][3][:])
+
+        pick_result(0, 0, pos1_sb)
+        pick_result(0, 1, pos2_sb)
+        add_shared(0)
+        pick_result(1, 0, pos1_sb)
+        add_second(0)
+        pick_result(1, 1, pos2_sb)
+        add_shared(1)
+        add_second(1)

@@ -74,6 +74,11 @@ def tile_moe_shr_lin_silu_kernel(tc, xT, w, b, gate, offs, pos1, pos2, out):
         def make_pairs(copy, g, u, a, z):
             copy(out=pairs[g][:, u, a:z, :], in_=x_raw[g][:, 2 * u : 2 * u + 2, a:z].rearrange("p t n -> p n t"))
 
+        def make_pairs_gpsimd(g, u, a, z):
+            nc.gpsimd.tensor_scalar(
+                pairs[g][:, u, a:z, :], x_raw[g][:, 2 * u : 2 * u + 2, a:z].rearrange("p t n -> p n t"), 1.0, 0.0, MULT, ADD
+            )
+
         def pick(g, u, i):
             s = slice(i * CUT, (i + 1) * CUT)
             window = pairs[g][:, u].rearrange("p n t -> p (n t)").bitcast(U32)
@@ -130,10 +135,12 @@ def tile_moe_shr_lin_silu_kernel(tc, xT, w, b, gate, offs, pos1, pos2, out):
         for i in range(CUTS):
             pick(0, 0, i)
         make_pairs(A, 0, 1, 0, T)
-        make_pairs(A, 1, 0, 0, T)
-        make_pairs(A, 1, 1, 0, T)
+        for u in range(2):
+            for a in range(0, T, 256):
+                make_pairs_gpsimd(1, u, a, a + 256)
         for i in range(CUTS):
             pick(0, 1, i)
+        weave(A, toks, 0, pairs[0], 0, T)
         spread_w(A, 0)
         weave(A, slots[0], 0, picked[0], 0, 1024)
         weave(A, slots[0], 0, picked[0], 1024, S)
@@ -149,16 +156,16 @@ def tile_moe_shr_lin_silu_kernel(tc, xT, w, b, gate, offs, pos1, pos2, out):
         spread_w(A, 3)
         pick(1, 0, 2)
         pick(1, 1, 2)
-        for e in range(4, E + 1):
-            spread_w(A, e)
-        weave(A, toks, 0, pairs[0], 0, T)
-        weave(A, toks, T, pairs[1], 0, T)
-        weave(V, slots[1], 0, picked[1], 512, 1024)
+        weave(A, slots[1], 0, picked[1], 512, 1024)
+        spread_w(A, 4)
+        spread_w(A, 5)
         quantise_w(0, 4)
+        weave(A, toks, T, pairs[1], 0, T)
+        weave(V, slots[1], 0, picked[1], 1024, S)
+        spread_w(A, E)
         quantise_slots(1, 0, 1024)
         for e in range(4):
             expert(e)
-        weave(V, slots[1], 0, picked[1], 1024, S)
         quantise_w(4, E)
         quantise_slots(1, 1024, S)
         for e in range(4, E):

from contextlib import ExitStack

import concourse.mybir as mybir

K, T, E, C, N = 1024, 768, 6, 256, 128
S = E * C
P = 128
GROUPS = K // 512
FLOPS = 2 * K * N * (S + T)

F32 = mybir.dt.float32
BF16 = mybir.dt.bfloat16
U32 = mybir.dt.uint32
U16 = mybir.dt.uint16
U8 = mybir.dt.uint8
FP8X4 = mybir.dt.float8_e4m3fn_x4
ADD = mybir.AluOpType.add
MULT = mybir.AluOpType.mult
SILU = mybir.ActivationFunctionType.Silu

CUT = 512
CUTS = S // CUT
HALF = T // 2


def tile_moe_shr_lin_silu_kernel(tc, xT, w, b, gate, offs, pos1, pos2, out):
    nc = tc.nc
    with ExitStack() as ctx:
        keep = ctx.enter_context(tc.tile_pool(name="keep", bufs=1))
        psum = ctx.enter_context(tc.psum_pool(name="psum", bufs=1))

        offs_sb = keep.tile([P, S // 16], U16, name="offs_sb")
        pos1_sb = keep.tile([P, T // 16], U16, name="pos1_sb")
        pos2_sb = keep.tile([P, T // 16], U16, name="pos2_sb")
        b_sb = keep.tile([P, E + 1], F32, name="b_sb")
        gate_sb = [keep.tile([P, T], F32, name=f"gate{r}") for r in range(2)]
        x_raw = [keep.tile([P, 4, T], F32, name=f"x_raw{g}") for g in range(GROUPS)]
        w_raw = [keep.tile([P, GROUPS, 4, N], F32, name=f"w_raw{e}") for e in range(E + 1)]
        pairs = [keep.tile([P, 2, T, 2], BF16, name=f"pairs{g}") for g in range(GROUPS)]
        picked = [keep.tile([P, 2, S, 2], BF16, name=f"picked{g}") for g in range(GROUPS)]
        slots = [keep.tile([P, S, 4], BF16, align_bytes=64, name=f"slots{g}") for g in range(GROUPS)]
        slot_codes = [keep.tile([P, S], U32, align_bytes=64, name=f"slot_codes{g}") for g in range(GROUPS)]
        slot_scales = [keep.tile([P, S], U8, align_bytes=64, name=f"slot_scales{g}") for g in range(GROUPS)]
        toks = keep.tile([P, GROUPS * T, 4], BF16, align_bytes=64, name="toks")
        tok_codes = keep.tile([P, GROUPS * T], U32, align_bytes=64, name="tok_codes")
        tok_scales = keep.tile([P, GROUPS * T], U8, align_bytes=64, name="tok_scales")
        w_bf = keep.tile([P, (E + 1) * GROUPS * N, 4], BF16, align_bytes=64, name="w_bf")
        w_codes = keep.tile([P, (E + 1) * GROUPS * N], U32, align_bytes=64, name="w_codes")
        w_scales = keep.tile([P, (E + 1) * GROUPS * N], U8, align_bytes=64, name="w_scales")
        y = keep.tile([P, S], F32, name="y")
        ys = keep.tile([P, T], F32, name="ys")
        warm = keep.tile([P, 1], F32, name="warm")
        acc = [psum.tile([P, C], F32, name=f"acc{e}") for e in range(E)]
        acc_s = [psum.tile([P, n], F32, name=f"acc_s{n}") for n in (512, 256)]

        nc.sync.dma_start(out=offs_sb[:], in_=offs)
        x_rows = xT.rearrange("(g p j) t -> g p j t", g=GROUPS, j=4)
        w_rows = w.rearrange("e (g p j) n -> e p g j n", g=GROUPS, j=4)
        for g in range(GROUPS):
            for u in range(2):
                for a, z in ((0, HALF), (HALF, T)) if g + u == 0 else ((0, T),):
                    nc.sync.dma_start(out=x_raw[g][:, 2 * u : 2 * u + 2, a:z], in_=x_rows[g, :, 2 * u : 2 * u + 2, a:z])
        for e in range(E + 1):
            nc.sync.dma_start(out=w_raw[e][:], in_=w_rows[e])
        nc.sync.dma_start(out=b_sb[:], in_=b)
        nc.sync.dma_start(out=pos1_sb[:], in_=pos1)
        nc.sync.dma_start(out=pos2_sb[:], in_=pos2)
        for r in range(2):
            nc.sync.dma_start(out=gate_sb[r][:], in_=gate[r])

        nc.vector.memset(warm[:], 0.0)
        nc.scalar.activation(warm[:], warm[:], SILU)

        def make_pairs(copy, g, u, a, z):
            copy(out=pairs[g][:, u, a:z, :], in_=x_raw[g][:, 2 * u : 2 * u + 2, a:z].rearrange("p t n -> p n t"))

        def make_pairs_gpsimd(g, u, a, z):
            nc.gpsimd.tensor_scalar(
                pairs[g][:, u, a:z, :], x_raw[g][:, 2 * u : 2 * u + 2, a:z].rearrange("p t n -> p n t"), 1.0, 0.0, MULT, ADD
            )

        def pick(g, u, i):
            s = slice(i * CUT, (i + 1) * CUT)
            window = pairs[g][:, u].rearrange("p n t -> p (n t)").bitcast(U32)
            into = picked[g][:, u, s, :].rearrange("p s t -> p (s t)").bitcast(U32)
            nc.vector.tensor_copy(into, window.indirect(offs_sb[:, i * CUT // 16 : (i + 1) * CUT // 16]))

        def weave(copy, into, b0, planes, a, z):
            copy(
                out=into[:, b0 + a : b0 + z, :].rearrange("p s t -> p (s t)").bitcast(F32).rearrange("p (s u) -> p s u", u=2),
                in_=planes[:].rearrange("p u s t -> p (u s t)").bitcast(F32).rearrange("p (u s) -> p s u", u=2)[:, a:z, :],
            )

        def quantise(values, codes, scales, a, z):
            nc.vector.quantize_mx(
                out=codes[:, a:z].bitcast(FP8X4),
                scales=scales[:, a:z],
                in_=values[:, a:z, :].rearrange("p s t -> p (s t)"),
            )

        def quantise_slots(g, a, z):
            quantise(slots[g], slot_codes[g], slot_scales[g], a, z)

        def quantise_w(a, z):
            quantise(w_bf, w_codes, w_scales, a * GROUPS * N, z * GROUPS * N)

        def spread_w(copy, e):
            c = e * GROUPS * N
            copy(
                out=w_bf[:, c : c + GROUPS * N, :].rearrange("p (g c i) t -> p g c t i", g=GROUPS, i=4),
                in_=w_raw[e][:].rearrange("p g t (c i) -> p g c t i", i=4),
            )

        def multiply(bank, e, g, codes, scales, cols):
            c = slice((e * GROUPS + g) * N, (e * GROUPS + g + 1) * N)
            nc.tensor.matmul_mx(
                out=bank,
                lhsT=w_codes[:, c].bitcast(FP8X4),
                lhsT_scale=w_scales[:, c],
                rhs=codes[:, cols].bitcast(FP8X4),
                rhs_scale=scales[:, cols],
                start=(g == 0),
                stop=(g == GROUPS - 1),
            )

        def expert(e):
            s = slice(e * C, (e + 1) * C)
            for g in range(GROUPS):
                multiply(acc[e][:], e, g, slot_codes[g], slot_scales[g], s)
            nc.scalar.activation(y[:, s], acc[e][:], SILU, bias=b_sb[:, e : e + 1])

        V, A = nc.vector.tensor_copy, nc.scalar.copy
        make_pairs(A, 0, 0, 0, HALF)
        make_pairs(V, 0, 0, HALF, T)
        for i in range(CUTS):
            pick(0, 0, i)
        make_pairs(A, 0, 1, 0, T)
        for u in range(2):
            for a in range(0, T, 256):
                make_pairs_gpsimd(1, u, a, a + 256)
        for i in range(CUTS):
            pick(0, 1, i)
        weave(A, toks, 0, pairs[0], 0, T)
        spread_w(A, 0)
        weave(A, slots[0], 0, picked[0], 0, 1024)
        weave(A, slots[0], 0, picked[0], 1024, S)
        pick(1, 0, 0)
        pick(1, 1, 0)
        for e in range(1, 3):
            spread_w(A, e)
        quantise_slots(0, 0, 1024)
        pick(1, 0, 1)
        quantise_slots(0, 1024, S)
        pick(1, 1, 1)
        weave(A, slots[1], 0, picked[1], 0, 512)
        spread_w(A, 3)
        pick(1, 0, 2)
        pick(1, 1, 2)
        weave(A, slots[1], 0, picked[1], 512, 1024)
        spread_w(A, 4)
        spread_w(A, 5)
        quantise_w(0, 4)
        weave(A, toks, T, pairs[1], 0, T)
        weave(V, slots[1], 0, picked[1], 1024, S)
        spread_w(A, E)
        quantise_slots(1, 0, 1024)
        for e in range(4):
            expert(e)
        quantise_w(4, E)
        quantise_slots(1, 1024, S)
        for e in range(4, E):
            expert(e)
        quantise(toks, tok_codes, tok_scales, 0, 1024)
        quantise(toks, tok_codes, tok_scales, 1024, GROUPS * T)
        quantise_w(E, E + 1)
        for h, (a, z) in enumerate(((0, 512), (512, T))):
            for g in range(GROUPS):
                multiply(acc_s[h][:], E, g, tok_codes, tok_scales, slice(g * T + a, g * T + z))
            nc.scalar.activation(ys[:, a:z], acc_s[h][:], SILU, bias=b_sb[:, E : E + 1])

        bounds = ((0, 512), (512, T))
        parts = []
        for h, (a, z) in enumerate(bounds):
            parts.append([keep.tile([P, z - a], F32, name=f"part{h}{k}") for k in range(4)])

        def pick_result(h, r, pos_sb):
            a, z = bounds[h]
            nc.vector.tensor_tensor(parts[h][r][:], y[:].indirect(pos_sb[:, a // 16 : z // 16]), gate_sb[r][:, a:z], MULT)

        def add_shared(h):
            a, z = bounds[h]
            nc.vector.tensor_tensor(parts[h][2][:], parts[h][0][:], ys[:, a:z], ADD)

        def add_second(h):
            a, z = bounds[h]
            nc.vector.tensor_tensor(parts[h][3][:], parts[h][2][:], parts[h][1][:], ADD)
            nc.sync.dma_start(out=out[:, a:z], in_=parts[h][3][:])

        pick_result(0, 0, pos1_sb)
        pick_result(0, 1, pos2_sb)
        add_shared(0)
        pick_result(1, 0, pos1_sb)
        add_second(0)
        pick_result(1, 1, pos2_sb)
        add_shared(1)
        add_second(1)
